import numpy as np
import ml_dtypes


def mxq(x, axis, fmt="e4m3"):
    dtype, down = {"e4m3": (ml_dtypes.float8_e4m3fn, 7), "e5m2": (ml_dtypes.float8_e5m2, 14)}[fmt]
    v = np.moveaxis(np.asarray(x, np.float32).astype(ml_dtypes.bfloat16).astype(np.float64), axis, -1)
    blocks = v.reshape(v.shape[:-1] + (-1, 32))
    amax = np.abs(blocks).max(-1, keepdims=True)
    byte = np.maximum(np.where(amax > 0, np.frexp(amax)[1] - 1 + 127, 0) - down, 1)
    scale = np.exp2(byte - 127.0)
    codes = (blocks / scale).astype(np.float32).astype(dtype).astype(np.float64)
    return np.moveaxis((codes * scale).reshape(v.shape), -1, axis)


WIDE = False


def mx_kscale(k):
    if not WIDE:
        return np.ones(k)
    levels = np.array([30, -30])
    if k % 512:
        return np.exp2(np.random.permutation(np.resize(levels, k // 32))).repeat(32)
    a = np.empty((k // 512, 16))
    for p in range(k // 512):
        a[p, :8] = np.random.permutation(np.resize(levels, 8))
        for g in range(8):
            far = levels[np.abs(levels - a[p, g]) >= 10]
            a[p, g + 8] = far[np.random.randint(len(far))]
    return np.exp2(a.ravel()).repeat(32)


def f64(x):
    return np.asarray(x).astype(np.float64)


def striped(idx):
    return np.tile(idx.reshape(-1, 16).T, (8, 1)).astype(np.uint16)


def unstriped(offs):
    return offs[:16].T.reshape(-1).astype(np.int64)


def d_relu(v):
    return (v > 0).astype(np.float64)


K, T, E, C, H, N = 128, 1024, 4, 512, 512, 1536


def by_expert(wq, xq):
    return np.concatenate([wq[e].T @ xq[:, e * C:(e + 1) * C] for e in range(E)], axis=1)


def setup_inputs():
    n = np.random.standard_normal
    s = mx_kscale(N)[:, None]
    u = mx_kscale(H)
    first = np.random.permutation(np.repeat(np.arange(E), T // E))
    second = (first + 1 + np.random.permutation(np.repeat(np.arange(E - 1), -(-T // (E - 1)))[:T])) % E
    while np.bincount(second, minlength=E).max() != T // E:
        load = np.bincount(second, minlength=E); hi, lo = int(load.argmax()), int(load.argmin())
        t = np.flatnonzero((second == hi) & (first != lo))[0]; second[t] = lo
    slot_token = np.empty(E * C, np.int64); pos = np.empty((2, T), np.int64); fill = np.zeros(E, np.int64)
    place = np.stack([np.random.permutation(C) for _ in range(E)])
    for r, deal in enumerate((first, second)):
        for t in np.random.permutation(T):
            e = deal[t]; j = e * C + place[e, fill[e]]; fill[e] += 1; slot_token[j] = t; pos[r, t] = j
    g = np.random.uniform(0.2, 0.8, T)
    w_slot = np.empty(E * C); w_slot[pos[0]] = g; w_slot[pos[1]] = 1.0 - g
    return {
        "dyT": (n((N, T)) * s).astype(np.float32),
        "a": n((H, E * C)).astype(np.float32),
        "w2": (n((E, N, H)) / np.sqrt(N) / s[None] * u[None, None, :]).astype(np.float32),
        "w1": (n((E, H, K)) / np.sqrt(H) / u[None, :, None]).astype(np.float32),
        "gate": np.tile(w_slot, (N, 1)).astype(np.float32),
        "offs": striped(slot_token),
        "pos1": striped(pos[0]),
        "pos2": striped(pos[1]),
    }


def reference(dyT, a, w2, w1, gate, offs, pos1, pos2):
    idx = unstriped(offs)
    gq = mxq(f64(gate) * f64(dyT)[:, idx], 0, "e5m2")
    dh = by_expert(mxq(f64(w2), 1, "e4m3"), gq)
    da = dh * d_relu(f64(a))
    dx = by_expert(mxq(f64(w1), 1, "e4m3"), mxq(da, 0, "e5m2"))
    return dx[:, unstriped(pos1)] + dx[:, unstriped(pos2)]

@@ -1,0 +1,255 @@
+from contextlib import ExitStack
+
+import concourse.mybir as mybir
+
+N, T, E, C, H, K = 1536, 1024, 4, 512, 512, 128
+
+F32 = mybir.dt.float32
+BF16 = mybir.dt.bfloat16
+U32 = mybir.dt.uint32
+U16 = mybir.dt.uint16
+U8 = mybir.dt.uint8
+E4M3 = mybir.dt.float8_e4m3fn_x4
+E5M2 = mybir.dt.float8_e5m2_x4
+MULT = mybir.AluOpType.mult
+IS_GT = mybir.AluOpType.is_gt
+
+FLOPS = 2 * E * C * H * (N + K)
+BYTES = 4 * (N * T + H * E * C + E * N * H + E * H * K + E * C + K * T) + 2 * (128 * 128 + 2 * 128 * 64)
+
+P = 128
+PACK = 4
+PASSES = N // (P * PACK)
+COLS = C // 16
+
+
+def tile_moe_bdx_mlp_relu_kernel(tc, dyT, a, w2, w1, gate, offs, pos1, pos2, out):
+    nc = tc.nc
+    units = [(e, c) for e in range(E) for c in range(PASSES)]
+    n_units = len(units)
+
+    with ExitStack() as ctx:
+        keep = ctx.enter_context(tc.tile_pool(name="keep", bufs=1))
+        planes = ctx.enter_context(tc.tile_pool(name="planes", bufs=4))
+        loads = ctx.enter_context(tc.tile_pool(name="loads", bufs=3))
+        pairs = ctx.enter_context(tc.tile_pool(name="pairs", bufs=2))
+        wring = ctx.enter_context(tc.tile_pool(name="wring", bufs=4))
+        psum_h = ctx.enter_context(tc.psum_pool(name="psum_h", bufs=7))
+        psum_x = ctx.enter_context(tc.psum_pool(name="psum_x", bufs=1))
+
+        offs_t = keep.tile([P, E * COLS], U16, name="offs_t")
+        pos1_t = keep.tile([P, T // 16], U16, name="pos1_t")
+        pos2_t = keep.tile([P, T // 16], U16, name="pos2_t")
+        gate_t = keep.tile([P, E * C], F32, name="gate_t")
+        dx_t = keep.tile([P, E * C], F32, name="dx_t")
+        nc.sync.dma_start(offs_t[:], offs)
+        nc.scalar.dma_start(out=gate_t[:, 0:C], in_=gate[0:P, 0:C])
+        dy_rows = dyT.rearrange("(c p j) t -> c p j t", c=PASSES, j=PACK)
+        dy = {}
+        for c in range(PASSES):
+            for j in range(PACK):
+                dy[c, j] = keep.tile([P, T], F32, name="dy_%d_%d" % (c, j))
+                nc.sync.dma_start(out=dy[c, j][:], in_=dy_rows[c, :, j, :])
+            if c == 0:
+                nc.sync.dma_start(out=gate_t[:, C:], in_=gate[0:P, C:])
+
+        w2_rows = w2.rearrange("e (c p j) i -> e c p j i", c=PASSES, j=PACK)
+        w2_raw = {}
+
+        def load_w2(u):
+            e, c = units[u]
+            w2_raw[u] = loads.tile([P, PACK, H], F32, name="w_raw")
+            nc.sync.dma_start(out=w2_raw[u][:], in_=w2_rows[e, c])
+
+        a_rows = a.rearrange("(p t) n -> p t n", t=PACK)
+        a_t = {}
+
+        def load_a(e):
+            a_t[e] = pairs.tile([P, PACK, C], F32, name="a_e")
+            nc.sync.dma_start(out=a_t[e][:], in_=a_rows[:, :, e * C : (e + 1) * C])
+
+        g_planes, g_bf, g_codes, g_scales = {}, {}, {}, {}
+
+        def gather(u, lo, hi):
+            e, c = units[u]
+            if lo == 0:
+                g_planes[u] = planes.tile([P, PACK, C], F32, name="plane")
+            cols = slice(e * COLS + lo // 16, e * COLS + hi // 16)
+            for j in range(PACK):
+                nc.vector.tensor_tensor(
+                    g_planes[u][:, j, lo:hi],
+                    dy[c, j][:].indirect(offs_t[:, cols]),
+                    gate_t[:, e * C + lo : e * C + hi],
+                    MULT,
+                )
+
+        def round_g(u, lo, hi):
+            if lo == 0:
+                g_bf[u] = loads.tile([P, PACK * C], BF16, name="g_bf", align_bytes=64)
+            nc.scalar.copy(
+                g_bf[u][:, PACK * lo : PACK * hi].rearrange("p (c i t) -> p c t i", i=4, t=PACK),
+                g_planes[u][:, :, lo:hi].rearrange("p t (c i) -> p c t i", i=4),
+            )
+
+        def quant_g(u):
+            g_codes[u] = keep.tile([P, C], U32, name="g_codes_%d" % u, align_bytes=64)
+            g_scales[u] = keep.tile([P, C], U8, name="g_scales_%d" % u, align_bytes=64)
+            nc.vector.quantize_mx(out=g_codes[u][:].bitcast(E5M2), scales=g_scales[u][:], in_=g_bf[u][:])
+
+        w_bf, w_codes, w_scales = {}, {}, {}
+
+        def round_w2(u):
+            w_bf[u] = loads.tile([P, PACK * H], BF16, name="w_bf", align_bytes=64)
+            nc.scalar.copy(
+                w_bf[u][:].rearrange("p (t m j) -> p m j t", t=PACK, j=PACK),
+                w2_raw[u][:].rearrange("p j (m t) -> p m j t", t=PACK),
+            )
+
+        def quant_w2(u):
+            w_codes[u] = wring.tile([P, H], U32, name="w_codes", align_bytes=64)
+            w_scales[u] = wring.tile([P, H], U8, name="w_scales", align_bytes=64)
+            nc.vector.quantize_mx(out=w_codes[u][:].bitcast(E4M3), scales=w_scales[u][:], in_=w_bf[u][:])
+
+        banks = {}
+
+        def multiply(u):
+            e, c = units[u]
+            for t in range(PACK):
+                if c == 0:
+                    banks[e, t] = psum_h.tile([P, C], F32, name="dh")
+                m = slice(t * P, (t + 1) * P)
+                nc.tensor.matmul_mx(
+                    out=banks[e, t][:],
+                    lhsT=w_codes[u][:, m].bitcast(E4M3),
+                    lhsT_scale=w_scales[u][:, m],
+                    rhs=g_codes[u][:].bitcast(E5M2),
+                    rhs_scale=g_scales[u][:],
+                    start=(c == 0),
+                    stop=(c == PASSES - 1),
+                )
+
+        w1_codes = keep.tile([P, E * K], U32, name="w1_codes", align_bytes=64)
+        w1_scales = keep.tile([P, E * K], U8, name="w1_scales", align_bytes=64)
+        w1_tiles = {}
+
+        def load_w1():
+            w1_tiles["raw"] = loads.tile([P, E, PACK * K], F32, name="w_raw")
+            nc.sync.dma_start(out=w1_tiles["raw"][:], in_=w1.rearrange("e (p j) k -> p e (j k)", j=PACK))
+
+        def round_w1():
+            w1_tiles["bf"] = loads.tile([P, PACK * E * K], BF16, name="w_bf", align_bytes=64)
+            for e in range(E):
+                nc.scalar.copy(
+                    w1_tiles["bf"][:, e * PACK * K : (e + 1) * PACK * K].rearrange("p (c i j) -> p c j i", i=4, j=PACK),
+                    w1_tiles["raw"][:, e, :].rearrange("p (j c i) -> p c j i", j=PACK, i=4),
+                )
+
+        def quant_w1():
+            nc.vector.quantize_mx(out=w1_codes[:].bitcast(E4M3), scales=w1_scales[:], in_=w1_tiles["bf"][:])
+
+        da_planes, da_bf, da_codes, da_scales = {}, {}, {}, {}
+
+        def mask(e, lo, hi):
+            if lo == 0:
+                da_planes[e] = pairs.tile([P, PACK, C], BF16, name="da_planes")
+            for t in range(PACK):
+                nc.vector.scalar_tensor_tensor(
+                    da_planes[e][:, t, lo:hi], a_t[e][:, t, lo:hi], 0.0, banks[e, t][:, lo:hi], op0=IS_GT, op1=MULT
+                )
+
+        def group_da(e, lo, hi):
+            if lo == 0:
+                da_bf[e] = pairs.tile([P, PACK * C], BF16, name="da_bf", align_bytes=64)
+            nc.scalar.copy(
+                da_bf[e][:, PACK * lo : PACK * hi].rearrange("p (c i t) -> p c t i", i=8, t=PACK),
+                da_planes[e][:, :, lo:hi].rearrange("p t (c i) -> p c t i", i=8),
+            )
+
+        def quant_da(e):
+            da_codes[e] = pairs.tile([P, C], U32, name="da_codes", align_bytes=64)
+            da_scales[e] = pairs.tile([P, C], U8, name="da_scales", align_bytes=64)
+            nc.vector.quantize_mx(out=da_codes[e][:].bitcast(E5M2), scales=da_scales[e][:], in_=da_bf[e][:])
+
+        def last_product(e):
+            bank = psum_x.tile([P, C], F32, name="dx")
+            k = slice(e * K, (e + 1) * K)
+            nc.tensor.matmul_mx(
+                out=bank[:],
+                lhsT=w1_codes[:, k].bitcast(E4M3),
+                lhsT_scale=w1_scales[:, k],
+                rhs=da_codes[e][:].bitcast(E5M2),
+                rhs_scale=da_scales[e][:],
+                start=True,
+                stop=True,
+            )
+            nc.scalar.copy(dx_t[:, e * C : (e + 1) * C], bank[:])
+
+        W1 = n_units
+        order = [0, 1, 2, W1] + list(range(3, n_units))
+        w_steps = {3: [0, 1], 4: [2, W1], 5: [3, 4], 6: [5], 7: [6, 7], 8: [8], 9: [9, 10], 10: [11]}
+
+        def load_item(u):
+            if u == W1:
+                load_w1()
+            else:
+                load_w2(u)
+        da_steps = {6: 0, 8: 1, 11: 2}
+        for u in order[:3]:
+            load_item(u)
+        load_a(0)
+        pending = []
+        next_load = 3
+        multiplied = 0
+        for s in range(n_units):
+            halves = ((0, C),) if s < n_units - 1 else ((0, C // 2), (C // 2, C))
+            for lo, hi in halves:
+                gather(s, lo, hi)
+                round_g(s, lo, hi)
+            if s > 0:
+                quant_g(s - 1)
+            for u in pending:
+                if u == W1:
+                    quant_w1()
+                else:
+                    quant_w2(u)
+            ready = min(len(w_codes), len(g_codes))
+            for u in range(multiplied, ready):
+                multiply(u)
+            multiplied = ready
+            pending = w_steps.get(s, [])
+            for u in pending:
+                if u == W1:
+                    round_w1()
+                else:
+                    round_w2(u)
+                if next_load < len(order):
+                    load_item(order[next_load])
+                    next_load += 1
+            if s == 4:
+                load_a(1)
+            if s == 5:
+                nc.sync.dma_start(pos1_t[:], pos1)
+                nc.sync.dma_start(pos2_t[:], pos2)
+            if s in da_steps:
+                e = da_steps[s]
+                mask(e, 0, C)
+                group_da(e, 0, C)
+                quant_da(e)
+                last_product(e)
+                if e + 2 < E:
+                    load_a(e + 2)
+        quant_g(n_units - 1)
+        multiply(n_units - 1)
+        for lo, hi in ((0, C // 2), (C // 2, C)):
+            mask(E - 1, lo, hi)
+            group_da(E - 1, lo, hi)
+        quant_da(E - 1)
+        last_product(E - 1)
+
+        for half in range(2):
+            cols = slice(half * T // 32, (half + 1) * T // 32)
+            both = planes.tile([P, PACK, C], F32, name="plane")
+            nc.vector.tensor_copy(both[:, 0, :], dx_t[:].indirect(pos1_t[:, cols]))
+            nc.vector.tensor_copy(both[:, 1, :], dx_t[:].indirect(pos2_t[:, cols]))
+            nc.vector.tensor_tensor(both[:, 2, :], both[:, 0, :], both[:, 1, :], mybir.AluOpType.add)
+            nc.sync.dma_start(out=out[:, half * T // 2 : (half + 1) * T // 2], in_=both[:, 2, :])

@@ -21,6 +21,7 @@ P = 128
 PACK = 4
 PASSES = N // (P * PACK)
 COLS = C // 16
+PAD = 8
 
 
 def tile_moe_bdx_mlp_relu_kernel(tc, dyT, a, w2, w1, gate, offs, pos1, pos2, out):
@@ -30,7 +31,7 @@ def tile_moe_bdx_mlp_relu_kernel(tc, dyT, a, w2, w1, gate, offs, pos1, pos2, out
 
     with ExitStack() as ctx:
         keep = ctx.enter_context(tc.tile_pool(name="keep", bufs=1))
-        planes = ctx.enter_context(tc.tile_pool(name="planes", bufs=4))
+        planes = ctx.enter_context(tc.tile_pool(name="planes", bufs=2))
         loads = ctx.enter_context(tc.tile_pool(name="loads", bufs=3))
         pairs = ctx.enter_context(tc.tile_pool(name="pairs", bufs=2))
         wring = ctx.enter_context(tc.tile_pool(name="wring", bufs=4))
@@ -46,12 +47,12 @@ def tile_moe_bdx_mlp_relu_kernel(tc, dyT, a, w2, w1, gate, offs, pos1, pos2, out
         nc.scalar.dma_start(out=gate_t[:, 0:C], in_=gate[0:P, 0:C])
         dy_rows = dyT.rearrange("(c p j) t -> c p j t", c=PASSES, j=PACK)
         dy = {}
-        for c in range(PASSES):
+
+        def load_dy(c):
             for j in range(PACK):
-                dy[c, j] = keep.tile([P, T], F32, name="dy_%d_%d" % (c, j))
-                nc.sync.dma_start(out=dy[c, j][:], in_=dy_rows[c, :, j, :])
-            if c == 0:
-                nc.sync.dma_start(out=gate_t[:, C:], in_=gate[0:P, C:])
+                dy[c, j] = keep.tile([P, T + PAD], F32, name="dy_%d_%d" % (c, j))
+                nc.gpsimd.memset(dy[c, j][:, T:], 0.0)
+                nc.sync.dma_start(out=dy[c, j][:, 0:T], in_=dy_rows[c, :, j, :])
 
         w2_rows = w2.rearrange("e (c p j) i -> e c p j i", c=PASSES, j=PACK)
         w2_raw = {}
@@ -68,27 +69,24 @@ def tile_moe_bdx_mlp_relu_kernel(tc, dyT, a, w2, w1, gate, offs, pos1, pos2, out
             a_t[e] = pairs.tile([P, PACK, C], F32, name="a_e")
             nc.sync.dma_start(out=a_t[e][:], in_=a_rows[:, :, e * C : (e + 1) * C])
 
-        g_planes, g_bf, g_codes, g_scales = {}, {}, {}, {}
+        g_bf, g_codes, g_scales = {}, {}, {}
 
-        def gather(u, lo, hi):
-            e, c = units[u]
-            if lo == 0:
-                g_planes[u] = planes.tile([P, PACK, C], F32, name="plane")
-            cols = slice(e * COLS + lo // 16, e * COLS + hi // 16)
-            for j in range(PACK):
+        def gather(plane, c, js, base, lo, hi):
+            for j in js:
                 nc.vector.tensor_tensor(
-                    g_planes[u][:, j, lo:hi],
-                    dy[c, j][:].indirect(offs_t[:, cols]),
-                    gate_t[:, e * C + lo : e * C + hi],
+                    plane[:, j, lo - base : hi - base],
+                    dy[c, j][:].indirect(offs_t[:, lo // 16 : hi // 16]),
+                    gate_t[:, lo:hi],
                     MULT,
                 )
 
-        def round_g(u, lo, hi):
-            if lo == 0:
+        def round_g(plane, u, base, lo, hi):
+            first = units[u][0] * C
+            if lo == first:
                 g_bf[u] = loads.tile([P, PACK * C], BF16, name="g_bf", align_bytes=64)
             nc.scalar.copy(
-                g_bf[u][:, PACK * lo : PACK * hi].rearrange("p (c i t) -> p c t i", i=4, t=PACK),
-                g_planes[u][:, :, lo:hi].rearrange("p t (c i) -> p c t i", i=4),
+                g_bf[u][:, PACK * (lo - first) : PACK * (hi - first)].rearrange("p (c i t) -> p c t i", i=4, t=PACK),
+                plane[:, :, lo - base : hi - base].rearrange("p t (c i) -> p c t i", i=4),
             )
 
         def quant_g(u):
@@ -157,10 +155,10 @@ def tile_moe_bdx_mlp_relu_kernel(tc, dyT, a, w2, w1, gate, offs, pos1, pos2, out
                     da_planes[e][:, t, lo:hi], a_t[e][:, t, lo:hi], 0.0, banks[e, t][:, lo:hi], op0=IS_GT, op1=MULT
                 )
 
-        def group_da(e, lo, hi):
+        def group_da(e, lo, hi, copy):
             if lo == 0:
                 da_bf[e] = pairs.tile([P, PACK * C], BF16, name="da_bf", align_bytes=64)
-            nc.scalar.copy(
+            copy(
                 da_bf[e][:, PACK * lo : PACK * hi].rearrange("p (c i t) -> p c t i", i=8, t=PACK),
                 da_planes[e][:, :, lo:hi].rearrange("p t (c i) -> p c t i", i=8),
             )
@@ -182,40 +180,74 @@ def tile_moe_bdx_mlp_relu_kernel(tc, dyT, a, w2, w1, gate, offs, pos1, pos2, out
                 start=True,
                 stop=True,
             )
-            nc.scalar.copy(dx_t[:, e * C : (e + 1) * C], bank[:])
+            if e < E - 1:
+                nc.scalar.copy(dx_t[:, e * C : (e + 1) * C], bank[:])
+            else:
+                nc.vector.tensor_copy(dx_t[:, e * C : (e + 1) * C], bank[:])
 
         W1 = n_units
         order = [0, 1, 2, W1] + list(range(3, n_units))
-        w_steps = {3: [0, 1], 4: [2, W1], 5: [3, 4], 6: [5], 7: [6, 7], 8: [8], 9: [9, 10], 10: [11]}
+        half = C // 2
 
         def load_item(u):
             if u == W1:
                 load_w1()
             else:
                 load_w2(u)
-        da_steps = {6: 0, 8: 1, 11: 2}
-        for u in order[:3]:
-            load_item(u)
+
+        load_dy(0)
+        nc.sync.dma_start(out=gate_t[:, C:], in_=gate[0:P, C:])
+        load_item(order[0])
+        load_dy(1)
+        load_item(order[1])
+        load_dy(2)
+        load_item(order[2])
         load_a(0)
-        pending = []
         next_load = 3
+
+        whole = (0, 1, 2, 3)
+        steps = [
+            (0, whole, 0, ((0, C),), True, (0,)),
+            (0, whole, 0, ((C, 2 * C),), False, (3,)),
+            (1, (0, 1), 0, ((0, 2 * C),), True, ()),
+            (1, (2, 3), 0, ((0, 2 * C),), False, (1, 4)),
+            (2, (0, 1), 0, ((0, 2 * C),), True, ()),
+            (2, (2, 3), 0, ((0, 2 * C),), False, (2, 5)),
+            (0, (0, 1), 2 * C, ((2 * C, 4 * C),), True, ()),
+            (0, (2, 3), 2 * C, ((2 * C, 4 * C),), False, (6, 9)),
+            (1, (0, 1), 2 * C, ((2 * C, 4 * C),), True, ()),
+            (1, (2, 3), 2 * C, ((2 * C, 4 * C),), False, (7, 10)),
+            (2, whole, 2 * C, ((2 * C, 3 * C),), True, (8,)),
+            (2, whole, 2 * C, ((3 * C, 3 * C + half), (3 * C + half, 4 * C)), False, (11,)),
+        ]
+        w_steps = {1: [0], 2: [1], 3: [2], 4: [W1], 5: [3, 4], 6: [5], 7: [6, 7], 8: [8], 9: [9, 10], 10: [11]}
+        mask_steps = {7: 0, 9: 1}
         multiplied = 0
-        for s in range(n_units):
-            halves = ((0, C),) if s < n_units - 1 else ((0, C // 2), (C // 2, C))
-            for lo, hi in halves:
-                gather(s, lo, hi)
-                round_g(s, lo, hi)
-            if s > 0:
-                quant_g(s - 1)
+        pending = []
+        masked = []
+        rounded = [[], []]
+        for s, (c, js, base, spans, fresh, done) in enumerate(steps):
+            if fresh:
+                plane = planes.tile([P, PACK, 2 * C], F32, name="plane")
+            for lo, hi in spans:
+                gather(plane, c, js, base, lo, hi)
+                if len(spans) > 1:
+                    round_g(plane, done[0], base, lo, hi)
+            if len(spans) == 1:
+                for u in done:
+                    round_g(plane, u, base, units[u][0] * C, (units[u][0] + 1) * C)
+            for u in rounded[0]:
+                quant_g(u)
+            rounded = [rounded[1], list(done)]
             for u in pending:
                 if u == W1:
                     quant_w1()
                 else:
                     quant_w2(u)
-            ready = min(len(w_codes), len(g_codes))
-            for u in range(multiplied, ready):
-                multiply(u)
-            multiplied = ready
+            for u in range(multiplied, n_units):
+                if u == multiplied and u in w_codes and u in g_codes:
+                    multiply(u)
+                    multiplied += 1
             pending = w_steps.get(s, [])
             for u in pending:
                 if u == W1:
@@ -227,29 +259,40 @@ def tile_moe_bdx_mlp_relu_kernel(tc, dyT, a, w2, w1, gate, offs, pos1, pos2, out
                     next_load += 1
             if s == 4:
                 load_a(1)
-            if s == 5:
                 nc.sync.dma_start(pos1_t[:], pos1)
                 nc.sync.dma_start(pos2_t[:], pos2)
-            if s in da_steps:
-                e = da_steps[s]
-                mask(e, 0, C)
-                group_da(e, 0, C)
+            for e in masked:
                 quant_da(e)
                 last_product(e)
+            masked = []
+            if s in mask_steps:
+                e = mask_steps[s]
+                mask(e, 0, C)
+                group_da(e, 0, C, nc.scalar.copy)
+                masked = [e]
                 if e + 2 < E:
                     load_a(e + 2)
-        quant_g(n_units - 1)
-        multiply(n_units - 1)
-        for lo, hi in ((0, C // 2), (C // 2, C)):
-            mask(E - 1, lo, hi)
-            group_da(E - 1, lo, hi)
-        quant_da(E - 1)
-        last_product(E - 1)
+        quant_g(8)
+        multiply(8)
+        for u in range(multiplied + 1, n_units - 1):
+            multiply(u)
+        mask(2, 0, C)
+        group_da(2, 0, C, nc.scalar.copy)
+        quant_g(11)
+        multiply(11)
+        quant_da(2)
+        last_product(2)
+        mask(3, 0, C)
+        group_da(3, 0, C // 4, nc.scalar.copy)
+        group_da(3, C // 4, C, nc.vector.tensor_copy)
+        quant_da(3)
+        last_product(3)
 
-        for half in range(2):
-            cols = slice(half * T // 32, (half + 1) * T // 32)
-            both = planes.tile([P, PACK, C], F32, name="plane")
-            nc.vector.tensor_copy(both[:, 0, :], dx_t[:].indirect(pos1_t[:, cols]))
-            nc.vector.tensor_copy(both[:, 1, :], dx_t[:].indirect(pos2_t[:, cols]))
-            nc.vector.tensor_tensor(both[:, 2, :], both[:, 0, :], both[:, 1, :], mybir.AluOpType.add)
-            nc.sync.dma_start(out=out[:, half * T // 2 : (half + 1) * T // 2], in_=both[:, 2, :])
+        for h in range(2):
+            cols = slice(h * T // 32, (h + 1) * T // 32)
+            both = planes.tile([P, PACK, 2 * C], F32, name="plane")
+            nc.vector.tensor_copy(both[:, 0, 0:C], dx_t[:].indirect(pos1_t[:, cols]))
+            nc.vector.tensor_copy(both[:, 1, 0:C], dx_t[:].indirect(pos2_t[:, cols]))
+            engine = nc.gpsimd if h == 0 else nc.vector
+            engine.tensor_tensor(both[:, 2, 0:C], both[:, 0, 0:C], both[:, 1, 0:C], mybir.AluOpType.add)
+            nc.sync.dma_start(out=out[:, h * T // 2 : (h + 1) * T // 2], in_=both[:, 2, 0:C])

@@ -34,9 +34,8 @@ def tile_moe_bdx_mlp_relu_kernel(tc, dyT, a, w2, w1, gate, offs, pos1, pos2, out
         planes = ctx.enter_context(tc.tile_pool(name="planes", bufs=2))
         loads = ctx.enter_context(tc.tile_pool(name="loads", bufs=3))
         pairs = ctx.enter_context(tc.tile_pool(name="pairs", bufs=2))
-        wring = ctx.enter_context(tc.tile_pool(name="wring", bufs=4))
-        psum_h = ctx.enter_context(tc.psum_pool(name="psum_h", bufs=7))
-        psum_x = ctx.enter_context(tc.psum_pool(name="psum_x", bufs=1))
+        wring = ctx.enter_context(tc.tile_pool(name="wring", bufs=6))
+        psum = ctx.enter_context(tc.psum_pool(name="psum", bufs=8))
 
         offs_t = keep.tile([P, E * COLS], U16, name="offs_t")
         pos1_t = keep.tile([P, T // 16], U16, name="pos1_t")
@@ -80,19 +79,23 @@ def tile_moe_bdx_mlp_relu_kernel(tc, dyT, a, w2, w1, gate, offs, pos1, pos2, out
                     MULT,
                 )
 
-        def round_g(plane, u, base, lo, hi):
-            first = units[u][0] * C
-            if lo == first:
-                g_bf[u] = loads.tile([P, PACK * C], BF16, name="g_bf", align_bytes=64)
+        def round_g(plane, us, base):
+            tile = loads.tile([P, len(us) * PACK * C], BF16, name="g_bf", align_bytes=64, bufs=2)
+            lo = units[us[0]][0] * C - base
+            for u in us:
+                g_bf[u] = tile
             nc.scalar.copy(
-                g_bf[u][:, PACK * (lo - first) : PACK * (hi - first)].rearrange("p (c i t) -> p c t i", i=4, t=PACK),
-                plane[:, :, lo - base : hi - base].rearrange("p t (c i) -> p c t i", i=4),
+                tile[:].rearrange("p (c i t) -> p c t i", i=4, t=PACK),
+                plane[:, :, lo : lo + len(us) * C].rearrange("p t (c i) -> p c t i", i=4),
             )
 
-        def quant_g(u):
-            g_codes[u] = keep.tile([P, C], U32, name="g_codes_%d" % u, align_bytes=64)
-            g_scales[u] = keep.tile([P, C], U8, name="g_scales_%d" % u, align_bytes=64)
-            nc.vector.quantize_mx(out=g_codes[u][:].bitcast(E5M2), scales=g_scales[u][:], in_=g_bf[u][:])
+        def quant_g(us):
+            codes = keep.tile([P, len(us) * C], U32, name="g_codes_%d" % us[0], align_bytes=64)
+            scales = keep.tile([P, len(us) * C], U8, name="g_scales_%d" % us[0], align_bytes=64)
+            nc.vector.quantize_mx(out=codes[:].bitcast(E5M2), scales=scales[:], in_=g_bf[us[0]][:])
+            for n, u in enumerate(us):
+                g_codes[u] = codes[:, n * C : (n + 1) * C]
+                g_scales[u] = scales[:, n * C : (n + 1) * C]
 
         w_bf, w_codes, w_scales = {}, {}, {}
 
@@ -114,14 +117,14 @@ def tile_moe_bdx_mlp_relu_kernel(tc, dyT, a, w2, w1, gate, offs, pos1, pos2, out
             e, c = units[u]
             for t in range(PACK):
                 if c == 0:
-                    banks[e, t] = psum_h.tile([P, C], F32, name="dh")
+                    banks[e, t] = psum.tile([P, C], F32, name="bank")
                 m = slice(t * P, (t + 1) * P)
                 nc.tensor.matmul_mx(
                     out=banks[e, t][:],
                     lhsT=w_codes[u][:, m].bitcast(E4M3),
                     lhsT_scale=w_scales[u][:, m],
-                    rhs=g_codes[u][:].bitcast(E5M2),
-                    rhs_scale=g_scales[u][:],
+                    rhs=g_codes[u].bitcast(E5M2),
+                    rhs_scale=g_scales[u],
                     start=(c == 0),
                     stop=(c == PASSES - 1),
                 )
@@ -131,16 +134,18 @@ def tile_moe_bdx_mlp_relu_kernel(tc, dyT, a, w2, w1, gate, offs, pos1, pos2, out
         w1_tiles = {}
 
         def load_w1():
-            w1_tiles["raw"] = loads.tile([P, E, PACK * K], F32, name="w_raw")
-            nc.sync.dma_start(out=w1_tiles["raw"][:], in_=w1.rearrange("e (p j) k -> p e (j k)", j=PACK))
+            w1_tiles["raw"] = loads.tile([P, PACK, E * K], F32, name="w_raw")
+            for e in range(E):
+                nc.sync.dma_start(
+                    out=w1_tiles["raw"][:, :, e * K : (e + 1) * K], in_=w1[e].rearrange("(p j) k -> p j k", j=PACK)
+                )
 
         def round_w1():
             w1_tiles["bf"] = loads.tile([P, PACK * E * K], BF16, name="w_bf", align_bytes=64)
-            for e in range(E):
-                nc.scalar.copy(
-                    w1_tiles["bf"][:, e * PACK * K : (e + 1) * PACK * K].rearrange("p (c i j) -> p c j i", i=4, j=PACK),
-                    w1_tiles["raw"][:, e, :].rearrange("p (j c i) -> p c j i", j=PACK, i=4),
-                )
+            nc.scalar.copy(
+                w1_tiles["bf"][:].rearrange("p (c i j) -> p c j i", i=4, j=PACK),
+                w1_tiles["raw"][:].rearrange("p j (c i) -> p c j i", i=4),
+            )
 
         def quant_w1():
             nc.vector.quantize_mx(out=w1_codes[:].bitcast(E4M3), scales=w1_scales[:], in_=w1_tiles["bf"][:])
@@ -169,7 +174,7 @@ def tile_moe_bdx_mlp_relu_kernel(tc, dyT, a, w2, w1, gate, offs, pos1, pos2, out
             nc.vector.quantize_mx(out=da_codes[e][:].bitcast(E5M2), scales=da_scales[e][:], in_=da_bf[e][:])
 
         def last_product(e):
-            bank = psum_x.tile([P, C], F32, name="dx")
+            bank = psum.tile([P, C], F32, name="bank")
             k = slice(e * K, (e + 1) * K)
             nc.tensor.matmul_mx(
                 out=bank[:],
@@ -186,8 +191,7 @@ def tile_moe_bdx_mlp_relu_kernel(tc, dyT, a, w2, w1, gate, offs, pos1, pos2, out
                 nc.vector.tensor_copy(dx_t[:, e * C : (e + 1) * C], bank[:])
 
         W1 = n_units
-        order = [0, 1, 2, W1] + list(range(3, n_units))
-        half = C // 2
+        order = [0, 3, 1, 4, W1, 2, 5, 6, 9, 7, 10, 8, 11]
 
         def load_item(u):
             if u == W1:
@@ -197,57 +201,60 @@ def tile_moe_bdx_mlp_relu_kernel(tc, dyT, a, w2, w1, gate, offs, pos1, pos2, out
 
         load_dy(0)
         nc.sync.dma_start(out=gate_t[:, C:], in_=gate[0:P, C:])
-        load_item(order[0])
+        for u in order[:3]:
+            load_item(u)
         load_dy(1)
-        load_item(order[1])
-        load_dy(2)
-        load_item(order[2])
-        load_a(0)
         next_load = 3
 
         whole = (0, 1, 2, 3)
         steps = [
             (0, whole, 0, ((0, C),), True, (0,)),
             (0, whole, 0, ((C, 2 * C),), False, (3,)),
+            (0, (0, 1), 2 * C, ((2 * C, 4 * C),), True, ()),
+            (0, (2, 3), 2 * C, ((2 * C, 4 * C),), False, (6, 9)),
             (1, (0, 1), 0, ((0, 2 * C),), True, ()),
             (1, (2, 3), 0, ((0, 2 * C),), False, (1, 4)),
             (2, (0, 1), 0, ((0, 2 * C),), True, ()),
             (2, (2, 3), 0, ((0, 2 * C),), False, (2, 5)),
-            (0, (0, 1), 2 * C, ((2 * C, 4 * C),), True, ()),
-            (0, (2, 3), 2 * C, ((2 * C, 4 * C),), False, (6, 9)),
             (1, (0, 1), 2 * C, ((2 * C, 4 * C),), True, ()),
             (1, (2, 3), 2 * C, ((2 * C, 4 * C),), False, (7, 10)),
             (2, whole, 2 * C, ((2 * C, 3 * C),), True, (8,)),
-            (2, whole, 2 * C, ((3 * C, 3 * C + half), (3 * C + half, 4 * C)), False, (11,)),
+            (2, whole, 2 * C, ((3 * C, 4 * C),), False, (11,)),
         ]
-        w_steps = {1: [0], 2: [1], 3: [2], 4: [W1], 5: [3, 4], 6: [5], 7: [6, 7], 8: [8], 9: [9, 10], 10: [11]}
-        mask_steps = {7: 0, 9: 1}
-        multiplied = 0
+        w_steps = {0: [0], 1: [3], 2: [1], 3: [4], 4: [W1], 5: [2], 6: [5, 6], 7: [9, 7], 8: [10, 8], 9: [11]}
+        products = {2: [0], 3: [3], 7: [1, 4], 9: [2, 5], 10: [6, 9]}
+        finish_steps = {10: (0, 1)}
         pending = []
-        masked = []
         rounded = [[], []]
         for s, (c, js, base, spans, fresh, done) in enumerate(steps):
             if fresh:
                 plane = planes.tile([P, PACK, 2 * C], F32, name="plane")
             for lo, hi in spans:
-                gather(plane, c, js, base, lo, hi)
-                if len(spans) > 1:
-                    round_g(plane, done[0], base, lo, hi)
-            if len(spans) == 1:
-                for u in done:
-                    round_g(plane, u, base, units[u][0] * C, (units[u][0] + 1) * C)
-            for u in rounded[0]:
-                quant_g(u)
-            rounded = [rounded[1], list(done)]
+                gather(plane, c, js[:1], base, lo, hi)
+                if s == n_units - 1:
+                    quant_g(rounded[0])
+                    for u in rounded[0]:
+                        multiply(u)
+                gather(plane, c, js[1:3], base, lo, hi)
+                if s == n_units - 1:
+                    quant_g(rounded[1])
+                    multiply(8)
+                gather(plane, c, js[3:], base, lo, hi)
+            if done:
+                round_g(plane, done, base)
+            if rounded[0] and s < n_units - 1:
+                quant_g(rounded[0])
+            rounded = [rounded[1], done]
             for u in pending:
                 if u == W1:
                     quant_w1()
                 else:
                     quant_w2(u)
-            for u in range(multiplied, n_units):
-                if u == multiplied and u in w_codes and u in g_codes:
-                    multiply(u)
-                    multiplied += 1
+            for e in finish_steps.get(s, ()):
+                quant_da(e)
+                last_product(e)
+            for u in products.get(s, ()):
+                multiply(u)
             pending = w_steps.get(s, [])
             for u in pending:
                 if u == W1:
@@ -257,28 +264,24 @@ def tile_moe_bdx_mlp_relu_kernel(tc, dyT, a, w2, w1, gate, offs, pos1, pos2, out
                 if next_load < len(order):
                     load_item(order[next_load])
                     next_load += 1
-            if s == 4:
+            if s == 1:
+                load_dy(2)
+            if s == 3:
+                load_a(0)
                 load_a(1)
+            if s == 4:
                 nc.sync.dma_start(pos1_t[:], pos1)
                 nc.sync.dma_start(pos2_t[:], pos2)
-            for e in masked:
-                quant_da(e)
-                last_product(e)
-            masked = []
-            if s in mask_steps:
-                e = mask_steps[s]
-                mask(e, 0, C)
-                group_da(e, 0, C, nc.scalar.copy)
-                masked = [e]
-                if e + 2 < E:
-                    load_a(e + 2)
-        quant_g(8)
-        multiply(8)
-        for u in range(multiplied + 1, n_units - 1):
-            multiply(u)
+            if s == 9:
+                mask(0, 0, C)
+                group_da(0, 0, C, nc.scalar.copy)
+                mask(1, 0, C)
+                group_da(1, 0, C, nc.scalar.copy)
+                load_a(2)
+                load_a(3)
         mask(2, 0, C)
         group_da(2, 0, C, nc.scalar.copy)
-        quant_g(11)
+        quant_g((11,))
         multiply(11)
         quant_da(2)
         last_product(2)
@@ -288,11 +291,12 @@ def tile_moe_bdx_mlp_relu_kernel(tc, dyT, a, w2, w1, gate, offs, pos1, pos2, out
         quant_da(3)
         last_product(3)
 
-        for h in range(2):
-            cols = slice(h * T // 32, (h + 1) * T // 32)
+        last = T * 5 // 8
+        for lo, hi, engine in ((0, last, nc.gpsimd), (last, T, nc.vector)):
+            cols = slice(lo // 16, hi // 16)
+            n = hi - lo
             both = planes.tile([P, PACK, 2 * C], F32, name="plane")
-            nc.vector.tensor_copy(both[:, 0, 0:C], dx_t[:].indirect(pos1_t[:, cols]))
-            nc.vector.tensor_copy(both[:, 1, 0:C], dx_t[:].indirect(pos2_t[:, cols]))
-            engine = nc.gpsimd if h == 0 else nc.vector
-            engine.tensor_tensor(both[:, 2, 0:C], both[:, 0, 0:C], both[:, 1, 0:C], mybir.AluOpType.add)
-            nc.sync.dma_start(out=out[:, h * T // 2 : (h + 1) * T // 2], in_=both[:, 2, 0:C])
+            nc.vector.tensor_copy(both[:, 0, 0:n], dx_t[:].indirect(pos1_t[:, cols]))
+            nc.vector.tensor_copy(both[:, 1, 0:n], dx_t[:].indirect(pos2_t[:, cols]))
+            engine.tensor_tensor(both[:, 2, 0:n], both[:, 0, 0:n], both[:, 1, 0:n], mybir.AluOpType.add)
+            nc.sync.dma_start(out=out[:, lo:hi], in_=both[:, 2, 0:n])

@@ -90,8 +90,9 @@ def tile_moe_bdx_mlp_relu_kernel(tc, dyT, a, w2, w1, gate, offs, pos1, pos2, out
             )
 
         def quant_g(us):
-            codes = keep.tile([P, len(us) * C], U32, name="g_codes_%d" % us[0], align_bytes=64)
-            scales = keep.tile([P, len(us) * C], U8, name="g_scales_%d" % us[0], align_bytes=64)
+            name, bufs = ("g_pair", 3) if len(us) == 2 else ("g_one", 4)
+            codes = keep.tile([P, len(us) * C], U32, name=name + "_codes", align_bytes=64, bufs=bufs)
+            scales = keep.tile([P, len(us) * C], U8, name=name + "_scales", align_bytes=64, bufs=bufs)
             nc.vector.quantize_mx(out=codes[:].bitcast(E5M2), scales=scales[:], in_=g_bf[us[0]][:])
             for n, u in enumerate(us):
                 g_codes[u] = codes[:, n * C : (n + 1) * C]
@@ -160,16 +161,33 @@ def tile_moe_bdx_mlp_relu_kernel(tc, dyT, a, w2, w1, gate, offs, pos1, pos2, out
                     da_planes[e][:, t, lo:hi], a_t[e][:, t, lo:hi], 0.0, banks[e, t][:, lo:hi], op0=IS_GT, op1=MULT
                 )
 
+        relu_mask = {}
+
+        def make_mask(e):
+            relu_mask[e] = keep.tile([P, PACK * C], BF16, name="relu_mask_%d" % e, align_bytes=64)
+            flat = relu_mask[e][:]
+            nc.scalar.activation(flat, a_t[e][:].rearrange("p t c -> p (t c)"), mybir.ActivationFunctionType.Sign)
+            nc.scalar.activation(flat, flat, mybir.ActivationFunctionType.Relu)
+
+        def empty_dh(e):
+            da_planes[e] = pairs.tile([P, PACK, C], BF16, name="da_planes")
+            for t in range(PACK):
+                nc.scalar.copy(da_planes[e][:, t, :], banks[e, t][:])
+
+        def apply_mask(e):
+            flat = da_planes[e][:].rearrange("p t c -> p (t c)")
+            nc.vector.tensor_tensor(flat, flat, relu_mask[e][:], MULT)
+
         def group_da(e, lo, hi, copy):
             if lo == 0:
-                da_bf[e] = pairs.tile([P, PACK * C], BF16, name="da_bf", align_bytes=64)
+                da_bf[e] = pairs.tile([P, PACK * C], BF16, name="da_bf", align_bytes=64, bufs=3)
             copy(
                 da_bf[e][:, PACK * lo : PACK * hi].rearrange("p (c i t) -> p c t i", i=8, t=PACK),
                 da_planes[e][:, :, lo:hi].rearrange("p t (c i) -> p c t i", i=8),
             )
 
         def quant_da(e):
-            da_codes[e] = pairs.tile([P, C], U32, name="da_codes", align_bytes=64)
+            da_codes[e] = pairs.tile([P, C], U32, name="da_codes", align_bytes=64, bufs=2)
             da_scales[e] = pairs.tile([P, C], U8, name="da_scales", align_bytes=64)
             nc.vector.quantize_mx(out=da_codes[e][:].bitcast(E5M2), scales=da_scales[e][:], in_=da_bf[e][:])
 
@@ -185,7 +203,7 @@ def tile_moe_bdx_mlp_relu_kernel(tc, dyT, a, w2, w1, gate, offs, pos1, pos2, out
                 start=True,
                 stop=True,
             )
-            if e < E - 1:
+            if e < 2:
                 nc.scalar.copy(dx_t[:, e * C : (e + 1) * C], bank[:])
             else:
                 nc.vector.tensor_copy(dx_t[:, e * C : (e + 1) * C], bank[:])
@@ -201,6 +219,7 @@ def tile_moe_bdx_mlp_relu_kernel(tc, dyT, a, w2, w1, gate, offs, pos1, pos2, out
 
         load_dy(0)
         nc.sync.dma_start(out=gate_t[:, C:], in_=gate[0:P, C:])
+        load_a(0)
         for u in order[:3]:
             load_item(u)
         load_dy(1)
@@ -223,7 +242,6 @@ def tile_moe_bdx_mlp_relu_kernel(tc, dyT, a, w2, w1, gate, offs, pos1, pos2, out
         ]
         w_steps = {0: [0], 1: [3], 2: [1], 3: [4], 4: [W1], 5: [2], 6: [5, 6], 7: [9, 7], 8: [10, 8], 9: [11]}
         products = {2: [0], 3: [3], 7: [1, 4], 9: [2, 5], 10: [6, 9]}
-        finish_steps = {10: (0, 1)}
         pending = []
         rounded = [[], []]
         for s, (c, js, base, spans, fresh, done) in enumerate(steps):
@@ -250,9 +268,6 @@ def tile_moe_bdx_mlp_relu_kernel(tc, dyT, a, w2, w1, gate, offs, pos1, pos2, out
                     quant_w1()
                 else:
                     quant_w2(u)
-            for e in finish_steps.get(s, ()):
-                quant_da(e)
-                last_product(e)
             for u in products.get(s, ()):
                 multiply(u)
             pending = w_steps.get(s, [])
@@ -265,15 +280,17 @@ def tile_moe_bdx_mlp_relu_kernel(tc, dyT, a, w2, w1, gate, offs, pos1, pos2, out
                     load_item(order[next_load])
                     next_load += 1
             if s == 1:
+                make_mask(0)
+            if s == 1:
                 load_dy(2)
             if s == 3:
-                load_a(0)
                 load_a(1)
             if s == 4:
                 nc.sync.dma_start(pos1_t[:], pos1)
                 nc.sync.dma_start(pos2_t[:], pos2)
             if s == 9:
-                mask(0, 0, C)
+                empty_dh(0)
+                apply_mask(0)
                 group_da(0, 0, C, nc.scalar.copy)
                 mask(1, 0, C)
                 group_da(1, 0, C, nc.scalar.copy)
@@ -283,13 +300,16 @@ def tile_moe_bdx_mlp_relu_kernel(tc, dyT, a, w2, w1, gate, offs, pos1, pos2, out
         group_da(2, 0, C, nc.scalar.copy)
         quant_g((11,))
         multiply(11)
-        quant_da(2)
-        last_product(2)
+        for e in (0, 1):
+            quant_da(e)
+            last_product(e)
         mask(3, 0, C)
         group_da(3, 0, C // 4, nc.scalar.copy)
         group_da(3, C // 4, C, nc.vector.tensor_copy)
         quant_da(3)
         last_product(3)
+        quant_da(2)
+        last_product(2)
 
         last = T * 5 // 8
         for lo, hi, engine in ((0, last, nc.gpsimd), (last, T, nc.vector)):

from contextlib import ExitStack

import concourse.mybir as mybir

N, T, E, C, H, K = 1536, 1024, 4, 512, 512, 128

F32 = mybir.dt.float32
BF16 = mybir.dt.bfloat16
U32 = mybir.dt.uint32
U16 = mybir.dt.uint16
U8 = mybir.dt.uint8
E4M3 = mybir.dt.float8_e4m3fn_x4
E5M2 = mybir.dt.float8_e5m2_x4
MULT = mybir.AluOpType.mult
IS_GT = mybir.AluOpType.is_gt

FLOPS = 2 * E * C * H * (N + K)
BYTES = 4 * (N * T + H * E * C + E * N * H + E * H * K + E * C + K * T) + 2 * (128 * 128 + 2 * 128 * 64)

P = 128
PACK = 4
PASSES = N // (P * PACK)
COLS = C // 16
PAD = 8


def tile_moe_bdx_mlp_relu_kernel(tc, dyT, a, w2, w1, gate, offs, pos1, pos2, out):
    nc = tc.nc
    units = [(e, c) for e in range(E) for c in range(PASSES)]
    n_units = len(units)

    with ExitStack() as ctx:
        keep = ctx.enter_context(tc.tile_pool(name="keep", bufs=1))
        planes = ctx.enter_context(tc.tile_pool(name="planes", bufs=2))
        loads = ctx.enter_context(tc.tile_pool(name="loads", bufs=3))
        pairs = ctx.enter_context(tc.tile_pool(name="pairs", bufs=2))
        wring = ctx.enter_context(tc.tile_pool(name="wring", bufs=6))
        psum = ctx.enter_context(tc.psum_pool(name="psum", bufs=8))

        offs_t = keep.tile([P, E * COLS], U16, name="offs_t")
        pos1_t = keep.tile([P, T // 16], U16, name="pos1_t")
        pos2_t = keep.tile([P, T // 16], U16, name="pos2_t")
        gate_t = keep.tile([P, E * C], F32, name="gate_t")
        dx_t = keep.tile([P, E * C], F32, name="dx_t")
        nc.sync.dma_start(offs_t[:], offs)
        nc.scalar.dma_start(out=gate_t[:, 0:C], in_=gate[0:P, 0:C])
        dy_rows = dyT.rearrange("(c p j) t -> c p j t", c=PASSES, j=PACK)
        dy = {}

        def load_dy(c):
            for j in range(PACK):
                dy[c, j] = keep.tile([P, T + PAD], F32, name="dy_%d_%d" % (c, j))
                nc.gpsimd.memset(dy[c, j][:, T:], 0.0)
                nc.sync.dma_start(out=dy[c, j][:, 0:T], in_=dy_rows[c, :, j, :])

        w2_rows = w2.rearrange("e (c p j) i -> e c p j i", c=PASSES, j=PACK)
        w2_raw = {}

        def load_w2(u):
            e, c = units[u]
            w2_raw[u] = loads.tile([P, PACK, H], F32, name="w_raw")
            nc.sync.dma_start(out=w2_raw[u][:], in_=w2_rows[e, c])

        a_rows = a.rearrange("(p t) n -> p t n", t=PACK)
        a_t = {}

        def load_a(e):
            a_t[e] = pairs.tile([P, PACK, C], F32, name="a_e")
            nc.sync.dma_start(out=a_t[e][:], in_=a_rows[:, :, e * C : (e + 1) * C])

        g_bf, g_codes, g_scales = {}, {}, {}

        def gather(plane, c, js, base, lo, hi):
            for j in js:
                nc.vector.tensor_tensor(
                    plane[:, j, lo - base : hi - base],
                    dy[c, j][:].indirect(offs_t[:, lo // 16 : hi // 16]),
                    gate_t[:, lo:hi],
                    MULT,
                )

        def round_g(plane, us, base):
            tile = loads.tile([P, len(us) * PACK * C], BF16, name="g_bf", align_bytes=64, bufs=2)
            lo = units[us[0]][0] * C - base
            for u in us:
                g_bf[u] = tile
            nc.scalar.copy(
                tile[:].rearrange("p (c i t) -> p c t i", i=4, t=PACK),
                plane[:, :, lo : lo + len(us) * C].rearrange("p t (c i) -> p c t i", i=4),
            )

        def quant_g(us):
            name, bufs = ("g_pair", 3) if len(us) == 2 else ("g_one", 4)
            codes = keep.tile([P, len(us) * C], U32, name=name + "_codes", align_bytes=64, bufs=bufs)
            scales = keep.tile([P, len(us) * C], U8, name=name + "_scales", align_bytes=64, bufs=bufs)
            nc.vector.quantize_mx(out=codes[:].bitcast(E5M2), scales=scales[:], in_=g_bf[us[0]][:])
            for n, u in enumerate(us):
                g_codes[u] = codes[:, n * C : (n + 1) * C]
                g_scales[u] = scales[:, n * C : (n + 1) * C]

        w_bf, w_codes, w_scales = {}, {}, {}

        def round_w2(u):
            w_bf[u] = loads.tile([P, PACK * H], BF16, name="w_bf", align_bytes=64)
            nc.scalar.copy(
                w_bf[u][:].rearrange("p (t m j) -> p m j t", t=PACK, j=PACK),
                w2_raw[u][:].rearrange("p j (m t) -> p m j t", t=PACK),
            )

        def quant_w2(u):
            w_codes[u] = wring.tile([P, H], U32, name="w_codes", align_bytes=64)
            w_scales[u] = wring.tile([P, H], U8, name="w_scales", align_bytes=64)
            nc.vector.quantize_mx(out=w_codes[u][:].bitcast(E4M3), scales=w_scales[u][:], in_=w_bf[u][:])

        banks = {}

        def multiply(u):
            e, c = units[u]
            for t in range(PACK):
                if c == 0:
                    banks[e, t] = psum.tile([P, C], F32, name="bank")
                m = slice(t * P, (t + 1) * P)
                nc.tensor.matmul_mx(
                    out=banks[e, t][:],
                    lhsT=w_codes[u][:, m].bitcast(E4M3),
                    lhsT_scale=w_scales[u][:, m],
                    rhs=g_codes[u].bitcast(E5M2),
                    rhs_scale=g_scales[u],
                    start=(c == 0),
                    stop=(c == PASSES - 1),
                )

        w1_codes = keep.tile([P, E * K], U32, name="w1_codes", align_bytes=64)
        w1_scales = keep.tile([P, E * K], U8, name="w1_scales", align_bytes=64)
        w1_tiles = {}

        def load_w1():
            w1_tiles["raw"] = loads.tile([P, PACK, E * K], F32, name="w_raw")
            for e in range(E):
                nc.sync.dma_start(
                    out=w1_tiles["raw"][:, :, e * K : (e + 1) * K], in_=w1[e].rearrange("(p j) k -> p j k", j=PACK)
                )

        def round_w1():
            w1_tiles["bf"] = loads.tile([P, PACK * E * K], BF16, name="w_bf", align_bytes=64)
            nc.scalar.copy(
                w1_tiles["bf"][:].rearrange("p (c i j) -> p c j i", i=4, j=PACK),
                w1_tiles["raw"][:].rearrange("p j (c i) -> p c j i", i=4),
            )

        def quant_w1():
            nc.vector.quantize_mx(out=w1_codes[:].bitcast(E4M3), scales=w1_scales[:], in_=w1_tiles["bf"][:])

        da_planes, da_bf, da_codes, da_scales = {}, {}, {}, {}

        def mask(e, lo, hi):
            if lo == 0:
                da_planes[e] = pairs.tile([P, PACK, C], BF16, name="da_planes")
            for t in range(PACK):
                nc.vector.scalar_tensor_tensor(
                    da_planes[e][:, t, lo:hi], a_t[e][:, t, lo:hi], 0.0, banks[e, t][:, lo:hi], op0=IS_GT, op1=MULT
                )

        relu_mask = {}

        def make_mask(e):
            relu_mask[e] = keep.tile([P, PACK * C], BF16, name="relu_mask_%d" % e, align_bytes=64)
            flat = relu_mask[e][:]
            nc.scalar.activation(flat, a_t[e][:].rearrange("p t c -> p (t c)"), mybir.ActivationFunctionType.Sign)
            nc.scalar.activation(flat, flat, mybir.ActivationFunctionType.Relu)

        def empty_dh(e):
            da_planes[e] = pairs.tile([P, PACK, C], BF16, name="da_planes")
            for t in range(PACK):
                nc.scalar.copy(da_planes[e][:, t, :], banks[e, t][:])

        def apply_mask(e):
            flat = da_planes[e][:].rearrange("p t c -> p (t c)")
            nc.vector.tensor_tensor(flat, flat, relu_mask[e][:], MULT)

        def group_da(e, lo, hi, copy):
            if lo == 0:
                da_bf[e] = pairs.tile([P, PACK * C], BF16, name="da_bf", align_bytes=64, bufs=3)
            copy(
                da_bf[e][:, PACK * lo : PACK * hi].rearrange("p (c i t) -> p c t i", i=8, t=PACK),
                da_planes[e][:, :, lo:hi].rearrange("p t (c i) -> p c t i", i=8),
            )

        def quant_da(e):
            da_codes[e] = pairs.tile([P, C], U32, name="da_codes", align_bytes=64, bufs=2)
            da_scales[e] = pairs.tile([P, C], U8, name="da_scales", align_bytes=64)
            nc.vector.quantize_mx(out=da_codes[e][:].bitcast(E5M2), scales=da_scales[e][:], in_=da_bf[e][:])

        def last_product(e):
            bank = psum.tile([P, C], F32, name="bank")
            k = slice(e * K, (e + 1) * K)
            nc.tensor.matmul_mx(
                out=bank[:],
                lhsT=w1_codes[:, k].bitcast(E4M3),
                lhsT_scale=w1_scales[:, k],
                rhs=da_codes[e][:].bitcast(E5M2),
                rhs_scale=da_scales[e][:],
                start=True,
                stop=True,
            )
            if e < 2:
                nc.scalar.copy(dx_t[:, e * C : (e + 1) * C], bank[:])
            else:
                nc.vector.tensor_copy(dx_t[:, e * C : (e + 1) * C], bank[:])

        W1 = n_units
        order = [0, 3, 1, 4, W1, 2, 5, 6, 9, 7, 10, 8, 11]

        def load_item(u):
            if u == W1:
                load_w1()
            else:
                load_w2(u)

        load_dy(0)
        nc.sync.dma_start(out=gate_t[:, C:], in_=gate[0:P, C:])
        load_a(0)
        for u in order[:3]:
            load_item(u)
        load_dy(1)
        next_load = 3

        whole = (0, 1, 2, 3)
        steps = [
            (0, whole, 0, ((0, C),), True, (0,)),
            (0, whole, 0, ((C, 2 * C),), False, (3,)),
            (0, (0, 1), 2 * C, ((2 * C, 4 * C),), True, ()),
            (0, (2, 3), 2 * C, ((2 * C, 4 * C),), False, (6, 9)),
            (1, (0, 1), 0, ((0, 2 * C),), True, ()),
            (1, (2, 3), 0, ((0, 2 * C),), False, (1, 4)),
            (2, (0, 1), 0, ((0, 2 * C),), True, ()),
            (2, (2, 3), 0, ((0, 2 * C),), False, (2, 5)),
            (1, (0, 1), 2 * C, ((2 * C, 4 * C),), True, ()),
            (1, (2, 3), 2 * C, ((2 * C, 4 * C),), False, (7, 10)),
            (2, whole, 2 * C, ((2 * C, 3 * C),), True, (8,)),
            (2, whole, 2 * C, ((3 * C, 4 * C),), False, (11,)),
        ]
        w_steps = {0: [0], 1: [3], 2: [1], 3: [4], 4: [W1], 5: [2], 6: [5, 6], 7: [9, 7], 8: [10, 8], 9: [11]}
        products = {2: [0], 3: [3], 7: [1, 4], 9: [2, 5], 10: [6, 9]}
        pending = []
        rounded = [[], []]
        for s, (c, js, base, spans, fresh, done) in enumerate(steps):
            if fresh:
                plane = planes.tile([P, PACK, 2 * C], F32, name="plane")
            for lo, hi in spans:
                gather(plane, c, js[:1], base, lo, hi)
                if s == n_units - 1:
                    quant_g(rounded[0])
                    for u in rounded[0]:
                        multiply(u)
                gather(plane, c, js[1:3], base, lo, hi)
                if s == n_units - 1:
                    quant_g(rounded[1])
                    multiply(8)
                gather(plane, c, js[3:], base, lo, hi)
            if done:
                round_g(plane, done, base)
            if rounded[0] and s < n_units - 1:
                quant_g(rounded[0])
            rounded = [rounded[1], done]
            for u in pending:
                if u == W1:
                    quant_w1()
                else:
                    quant_w2(u)
            for u in products.get(s, ()):
                multiply(u)
            pending = w_steps.get(s, [])
            for u in pending:
                if u == W1:
                    round_w1()
                else:
                    round_w2(u)
                if next_load < len(order):
                    load_item(order[next_load])
                    next_load += 1
            if s == 1:
                make_mask(0)
            if s == 1:
                load_dy(2)
            if s == 3:
                load_a(1)
            if s == 4:
                nc.sync.dma_start(pos1_t[:], pos1)
                nc.sync.dma_start(pos2_t[:], pos2)
            if s == 9:
                empty_dh(0)
                apply_mask(0)
                group_da(0, 0, C, nc.scalar.copy)
                mask(1, 0, C)
                group_da(1, 0, C, nc.scalar.copy)
                load_a(2)
                load_a(3)
        mask(2, 0, C)
        group_da(2, 0, C, nc.scalar.copy)
        quant_g((11,))
        multiply(11)
        for e in (0, 1):
            quant_da(e)
            last_product(e)
        mask(3, 0, C)
        group_da(3, 0, C // 4, nc.scalar.copy)
        group_da(3, C // 4, C, nc.vector.tensor_copy)
        quant_da(3)
        last_product(3)
        quant_da(2)
        last_product(2)

        last = T * 5 // 8
        for lo, hi, engine in ((0, last, nc.gpsimd), (last, T, nc.vector)):
            cols = slice(lo // 16, hi // 16)
            n = hi - lo
            both = planes.tile([P, PACK, 2 * C], F32, name="plane")
            nc.vector.tensor_copy(both[:, 0, 0:n], dx_t[:].indirect(pos1_t[:, cols]))
            nc.vector.tensor_copy(both[:, 1, 0:n], dx_t[:].indirect(pos2_t[:, cols]))
            engine.tensor_tensor(both[:, 2, 0:n], both[:, 0, 0:n], both[:, 1, 0:n], mybir.AluOpType.add)
            nc.sync.dma_start(out=out[:, lo:hi], in_=both[:, 2, 0:n])
